import numpy as np
import ml_dtypes


def mxq(x, axis, fmt="e4m3"):
    dtype, down = {"e4m3": (ml_dtypes.float8_e4m3fn, 7), "e5m2": (ml_dtypes.float8_e5m2, 14)}[fmt]
    v = np.moveaxis(np.asarray(x, np.float32).astype(ml_dtypes.bfloat16).astype(np.float64), axis, -1)
    blocks = v.reshape(v.shape[:-1] + (-1, 32))
    amax = np.abs(blocks).max(-1, keepdims=True)
    byte = np.maximum(np.where(amax > 0, np.frexp(amax)[1] - 1 + 127, 0) - down, 1)
    scale = np.exp2(byte - 127.0)
    codes = (blocks / scale).astype(np.float32).astype(dtype).astype(np.float64)
    return np.moveaxis((codes * scale).reshape(v.shape), -1, axis)


WIDE = False


def mx_kscale(k):
    if not WIDE:
        return np.ones(k)
    levels = np.array([30, -30])
    if k % 512:
        return np.exp2(np.random.permutation(np.resize(levels, k // 32))).repeat(32)
    a = np.empty((k // 512, 16))
    for p in range(k // 512):
        a[p, :8] = np.random.permutation(np.resize(levels, 8))
        for g in range(8):
            far = levels[np.abs(levels - a[p, g]) >= 10]
            a[p, g + 8] = far[np.random.randint(len(far))]
    return np.exp2(a.ravel()).repeat(32)


def f64(x):
    return np.asarray(x).astype(np.float64)


def striped(idx):
    return np.tile(np.asarray(idx).reshape(-1, 16).T, (8, 1)).astype(np.uint16)


def unstriped(offs):
    return offs[:16].T.reshape(-1).astype(np.int64)


E2M1 = np.array([0.0, 0.5, 1.0, 1.5, 2.0, 3.0, 4.0, 6.0, -0.0, -0.5, -1.0, -1.5, -2.0, -3.0, -4.0, -6.0])


def pack_weight(w, fmt):
    k, n = w.shape
    w = f64(np.asarray(w, np.float32).astype(ml_dtypes.bfloat16)).reshape(k // 32, 32, n)
    amax = np.abs(w).max(1)
    if fmt == "e4m3":
        byte = np.frexp(amax)[1] - 1 + 127 - 7
    else:
        mant, ex = np.frexp(amax / 6.0)
        byte = np.where(mant > 0.5, ex, ex - 1) + 127
    byte = np.clip(np.where(amax > 0, byte, 1), 1, 254)
    scaled = (w * np.exp2(127.0 - byte)[:, None, :]).reshape(k, n).astype(np.float32)
    by_word = np.ascontiguousarray(scaled.reshape(k // 512, 128, 4, n).transpose(0, 1, 3, 2))
    if fmt == "e4m3":
        words = by_word.astype(ml_dtypes.float8_e4m3fn).view(np.uint8)
    else:
        c = by_word.astype(ml_dtypes.float4_e2m1fn).view(np.uint8) & 0xF
        words = (c[..., 0::2] | (c[..., 1::2] << 4)).reshape(k // 512, 128, 2 * n)
    return np.ascontiguousarray(words), np.ascontiguousarray(byte.astype(np.uint8).reshape(k // 512, 16, n))


def unpack_weight(words, scales, fmt):
    g, _, n = scales.shape
    words = np.ascontiguousarray(words).reshape(g, 128, n, -1)
    if fmt == "e4m3":
        vals = words.view(ml_dtypes.float8_e4m3fn).astype(np.float64)
    else:
        nib = np.empty((g, 128, n, 4), np.uint8)
        nib[..., 0::2] = words & 0xF
        nib[..., 1::2] = words >> 4
        vals = E2M1[nib]
    vals = vals * np.repeat(np.exp2(scales.astype(np.float64) - 127.0), 8, axis=1)[..., None]
    return vals.transpose(0, 1, 3, 2).reshape(g * 512, n)


K, N, T, J = 512, 1024, 2048, 512


def setup_inputs():
    n = np.random.standard_normal
    idx = np.random.permutation(T)[:J]
    fn = mx_kscale(N)
    wp = pack_weight(n((N, K)) * 1 / np.sqrt(N) * fn[:, None], "e2m1")
    return {
        "g": (n((N, T)) * np.exp(0.5 * n((1, T))) / fn[:, None]).astype(np.float32),
        "w_words": wp[0],
        "w_scales": wp[1],
        "xh": (n((K, T))).astype(np.float32),
        "inv": (np.random.uniform(0.5, 2.0, (J, 1))).astype(np.float32),
        "offs": striped(idx),
    }


def reference(g, w_words, w_scales, xh, inv, offs):
    idx = unstriped(offs)
    wu = unpack_weight(w_words, w_scales, "e2m1")
    gidxq = mxq(f64(g)[:, idx], 0, "e5m2")
    gq = gidxq.T @ wu
    xj = f64(xh)[:, idx].T
    y = f64(inv) * (gq - xj * np.mean(gq * xj, axis=1, keepdims=True))
    return y

@@ -1,0 +1,152 @@
+from contextlib import ExitStack
+
+import concourse.mybir as mybir
+from concourse.masks import make_identity
+
+K, N, T, J = 512, 1024, 2048, 512
+FLOPS = 2 * J * N * K
+
+F32 = mybir.dt.float32
+BF16 = mybir.dt.bfloat16
+I32 = mybir.dt.int32
+U32 = mybir.dt.uint32
+U16 = mybir.dt.uint16
+U8 = mybir.dt.uint8
+E5M2X4 = mybir.dt.float8_e5m2_x4
+E2M1X4 = mybir.dt.float4_e2m1fn_x4
+MULT = mybir.AluOpType.mult
+ADD = mybir.AluOpType.add
+COPY = mybir.ActivationFunctionType.Copy
+
+P = 128
+PACK = 4
+PASSES = N // (P * PACK)
+TILES = J // P
+CHUNKS = K // P
+HALF = J // 2
+LIST_COLS = J // 16
+
+
+def tile_list_unit_size_back_kernel(tc, g, w_words, w_scales, xh, inv, offs, out):
+    nc = tc.nc
+    with ExitStack() as ctx:
+        keep = ctx.enter_context(tc.tile_pool(name="keep", bufs=1))
+        stage = ctx.enter_context(tc.tile_pool(name="stage", bufs=1))
+        psum = ctx.enter_context(tc.psum_pool(name="psum", bufs=1))
+
+        offsets = keep.tile([P, LIST_COLS], U16, name="offsets")
+        g_rows = g.rearrange("(a p i) t -> a i p t", a=PASSES, i=PACK)
+        g_sb = [[keep.tile([P, T], F32, name=f"g_{a}_{i}") for i in range(PACK)] for a in range(PASSES)]
+        xh_sb = [keep.tile([P, T], F32, name=f"xh_{c}") for c in range(CHUNKS)]
+        w_sb = keep.tile([P, PASSES, 2 * K], U8, name="w_sb", align_bytes=64)
+        w_sc = keep.tile([P, PASSES, K], U8, name="w_sc", align_bytes=64)
+        ident = keep.tile([P, P], F32, name="ident")
+        inv_rows = keep.tile([P, P], F32, name="inv_rows")
+        inv_cols = keep.tile([P, TILES], F32, name="inv_cols")
+
+        nc.vector.memset(w_sc[:].bitcast(I32), 0)
+        nc.vector.memset(inv_rows[:], 0.0)
+        make_identity(nc, ident[:])
+
+        nc.sync.dma_start(out=g_sb[0][0][:], in_=g_rows[0, 0])
+        nc.sync.dma_start(offsets[:], offs)
+        nc.sync.dma_start(out=inv_rows[0:TILES, :], in_=inv.rearrange("(t p) o -> t (p o)", p=P))
+        for q in range(4):
+            nc.sync.dma_start(
+                out=w_sc[32 * q:32 * q + 4, :, :].bitcast(I32),
+                in_=w_scales[:, 4 * q:4 * q + 4, :].rearrange("z r c -> r z c").bitcast(I32),
+            )
+        for i in range(1, PACK):
+            nc.sync.dma_start(out=g_sb[0][i][:], in_=g_rows[0, i])
+        nc.sync.dma_start(out=w_sb[:].bitcast(I32), in_=w_words.rearrange("z p b -> p z b").bitcast(I32))
+        for i in range(PACK):
+            nc.sync.dma_start(out=g_sb[1][i][:], in_=g_rows[1, i])
+        for c in range(CHUNKS):
+            nc.sync.dma_start(out=xh_sb[c][:], in_=xh[c * P:(c + 1) * P, :])
+
+        gq_ps = [psum.tile([P, K], F32, name=f"gq_ps{t}") for t in range(TILES)]
+        xj_ps = [psum.tile([P, K], F32, name=f"xj_ps{t}") for t in range(TILES)]
+
+        nc.tensor.transpose(xj_ps[0][:, 0:P], inv_rows[:], ident[:])
+        nc.vector.tensor_copy(out=inv_cols[:], in_=xj_ps[0][:, 0:TILES])
+
+        gqi = [keep.tile([P, K], F32, name=f"gqi{t}") for t in range(TILES)]
+        tile_cols = LIST_COLS // TILES
+        for a in range(PASSES):
+            picked = [keep.tile([P, PACK, P], BF16, name=f"picked_{a}_{t}") for t in range(TILES)]
+            woven = [stage.tile([P, P, PACK], BF16, name=f"woven_{a}_{t}", offset=(TILES - 1 - t) * 1024, align_bytes=64) for t in range(TILES)]
+            codes = [keep.tile([P, P], U32, name=f"codes_{a}_{t}", align_bytes=64) for t in range(TILES)]
+            scales = [keep.tile([P, P], U8, name=f"scales_{a}_{t}", align_bytes=64) for t in range(TILES)]
+            for i in range(PACK):
+                for t in range(TILES):
+                    window = g_sb[a][i][:].indirect(offsets[:, t * tile_cols:(t + 1) * tile_cols])
+                    if i == PACK - 1 and t == 0:
+                        nc.vector.tensor_copy(out=picked[t][:, i, :], in_=window)
+                    else:
+                        nc.scalar.activation(out=picked[t][:, i, :], in_=window, func=COPY)
+            for t in range(TILES):
+                nc.vector.tensor_copy(
+                    out=woven[t][:].rearrange("p (c e) i -> p c i e", e=4),
+                    in_=picked[t][:].rearrange("p i (c e) -> p c i e", e=4),
+                )
+                nc.vector.quantize_mx(
+                    out=codes[t][:].bitcast(E5M2X4),
+                    scales=scales[t][:],
+                    in_=woven[t][:].rearrange("p j i -> p (j i)"),
+                )
+                nc.tensor.matmul_mx(
+                    out=gq_ps[t][:],
+                    lhsT=codes[t][:].bitcast(E5M2X4),
+                    lhsT_scale=scales[t][:],
+                    rhs=w_sb[:, a, :].bitcast(E2M1X4),
+                    rhs_scale=w_sc[:, a, :],
+                    start=(a == 0),
+                    stop=(a == PASSES - 1),
+                )
+        for t in range(TILES):
+            nc.scalar.activation(out=gqi[t][:], in_=gq_ps[t][:], func=COPY, scale=inv_cols[:, t:t + 1])
+
+        out_sb = [keep.tile([P, K], F32, name=f"out_sb{t}") for t in range(TILES)]
+        parts = [keep.tile([P, TILES], F32, name=f"parts{n}") for n in range(3)]
+        early = keep.tile([P, TILES], F32, name="early")
+        coef = keep.tile([P, TILES], F32, name="coef")
+
+        def bring(c, vector_tiles):
+            xj_t = [stage.tile([P, P], F32, name=f"xj_t{c}_{t}", offset=t * 512, align_bytes=64) for t in range(TILES)]
+            for t in range(TILES):
+                window = xh_sb[c][:].indirect(offsets[:, t * tile_cols:(t + 1) * tile_cols])
+                if t < vector_tiles:
+                    nc.vector.tensor_copy(out=xj_t[t][:], in_=window)
+                else:
+                    nc.scalar.activation(out=xj_t[t][:], in_=window, func=COPY)
+            for t in range(TILES):
+                nc.tensor.transpose(xj_ps[t][:, c * P:(c + 1) * P], xj_t[t][:], ident[:])
+
+        def dot(t, ks, part):
+            nc.vector.scalar_tensor_tensor(
+                out=out_sb[t][:, ks], in0=xj_ps[t][:, ks], scalar=-1.0 / K, in1=gqi[t][:, ks],
+                op0=MULT, op1=MULT, accum_out=part[:, t:t + 1],
+            )
+
+        def total(t):
+            nc.vector.tensor_tensor(out=coef[:, t:t + 1], in0=early[:, t:t + 1], in1=parts[2][:, t:t + 1], op=ADD)
+
+        def finish(t):
+            nc.vector.scalar_tensor_tensor(
+                out=out_sb[t][:], in0=xj_ps[t][:], scalar=coef[:, t:t + 1], in1=gqi[t][:], op0=MULT, op1=ADD
+            )
+            nc.sync.dma_start(out=out[t * P:(t + 1) * P, :], in_=out_sb[t][:])
+
+        bring(0, 4)
+        bring(1, 2)
+        for t in range(TILES):
+            dot(t, slice(0, 2 * P), parts[0])
+        bring(2, 0)
+        for t in range(TILES):
+            dot(t, slice(2 * P, 3 * P), parts[1])
+        nc.vector.tensor_tensor(out=early[:], in0=parts[0][:], in1=parts[1][:], op=ADD)
+        bring(3, 0)
+        for t in range(TILES):
+            dot(t, slice(3 * P, 4 * P), parts[2])
+            total(t)
+            finish(t)

@@ -17,6 +17,7 @@ E2M1X4 = mybir.dt.float4_e2m1fn_x4
 MULT = mybir.AluOpType.mult
 ADD = mybir.AluOpType.add
 COPY = mybir.ActivationFunctionType.Copy
+IDENTITY = mybir.ActivationFunctionType.Identity
 
 P = 128
 PACK = 4
@@ -35,8 +36,10 @@ def tile_list_unit_size_back_kernel(tc, g, w_words, w_scales, xh, inv, offs, out
         psum = ctx.enter_context(tc.psum_pool(name="psum", bufs=1))
 
         offsets = keep.tile([P, LIST_COLS], U16, name="offsets")
-        g_rows = g.rearrange("(a p i) t -> a i p t", a=PASSES, i=PACK)
-        g_sb = [[keep.tile([P, T], F32, name=f"g_{a}_{i}") for i in range(PACK)] for a in range(PASSES)]
+        g_rows = g.rearrange("(a p i) t -> a p i t", a=PASSES, i=PACK)
+        g_first = keep.tile([P, PACK, T], F32, name="g_first")
+        g_pair = keep.tile([P, 2, T], F32, name="g_pair")
+        g_lone = [keep.tile([P, T], F32, name=f"g_lone{u}") for u in range(2)]
         xh_sb = [keep.tile([P, T], F32, name=f"xh_{c}") for c in range(CHUNKS)]
         w_sb = keep.tile([P, PASSES, 2 * K], U8, name="w_sb", align_bytes=64)
         w_sc = keep.tile([P, PASSES, K], U8, name="w_sc", align_bytes=64)
@@ -48,19 +51,18 @@ def tile_list_unit_size_back_kernel(tc, g, w_words, w_scales, xh, inv, offs, out
         nc.vector.memset(inv_rows[:], 0.0)
         make_identity(nc, ident[:])
 
-        nc.sync.dma_start(out=g_sb[0][0][:], in_=g_rows[0, 0])
+        nc.sync.dma_start(out=g_first[:], in_=g_rows[0])
         nc.sync.dma_start(offsets[:], offs)
+        nc.sync.dma_start(out=g_pair[:], in_=g_rows[1, :, 0:2, :])
         nc.sync.dma_start(out=inv_rows[0:TILES, :], in_=inv.rearrange("(t p) o -> t (p o)", p=P))
         for q in range(4):
             nc.sync.dma_start(
                 out=w_sc[32 * q:32 * q + 4, :, :].bitcast(I32),
                 in_=w_scales[:, 4 * q:4 * q + 4, :].rearrange("z r c -> r z c").bitcast(I32),
             )
-        for i in range(1, PACK):
-            nc.sync.dma_start(out=g_sb[0][i][:], in_=g_rows[0, i])
         nc.sync.dma_start(out=w_sb[:].bitcast(I32), in_=w_words.rearrange("z p b -> p z b").bitcast(I32))
-        for i in range(PACK):
-            nc.sync.dma_start(out=g_sb[1][i][:], in_=g_rows[1, i])
+        for u in range(2):
+            nc.sync.dma_start(out=g_lone[u][:], in_=g_rows[1, :, 2 + u, :])
         for c in range(CHUNKS):
             nc.sync.dma_start(out=xh_sb[c][:], in_=xh[c * P:(c + 1) * P, :])
 
@@ -72,37 +74,55 @@ def tile_list_unit_size_back_kernel(tc, g, w_words, w_scales, xh, inv, offs, out
 
         gqi = [keep.tile([P, K], F32, name=f"gqi{t}") for t in range(TILES)]
         tile_cols = LIST_COLS // TILES
-        for a in range(PASSES):
-            picked = [keep.tile([P, PACK, P], BF16, name=f"picked_{a}_{t}") for t in range(TILES)]
-            woven = [stage.tile([P, P, PACK], BF16, name=f"woven_{a}_{t}", offset=(TILES - 1 - t) * 1024, align_bytes=64) for t in range(TILES)]
-            codes = [keep.tile([P, P], U32, name=f"codes_{a}_{t}", align_bytes=64) for t in range(TILES)]
-            scales = [keep.tile([P, P], U8, name=f"scales_{a}_{t}", align_bytes=64) for t in range(TILES)]
-            for i in range(PACK):
-                for t in range(TILES):
-                    window = g_sb[a][i][:].indirect(offsets[:, t * tile_cols:(t + 1) * tile_cols])
-                    if i == PACK - 1 and t == 0:
-                        nc.vector.tensor_copy(out=picked[t][:, i, :], in_=window)
-                    else:
-                        nc.scalar.activation(out=picked[t][:, i, :], in_=window, func=COPY)
+
+        def gather(on_vector, dst, window):
+            if on_vector:
+                nc.vector.tensor_copy(out=dst, in_=window)
+            else:
+                nc.scalar.activation(out=dst, in_=window, func=COPY)
+
+        def quantise(picked, woven, name):
+            width = woven.shape[1]
+            codes = keep.tile([P, width], U32, name=f"codes_{name}", align_bytes=64)
+            scales = keep.tile([P, width], U8, name=f"scales_{name}", align_bytes=64)
+            nc.vector.tensor_copy(
+                out=woven[:].rearrange("p (c e) i -> p c i e", e=4),
+                in_=picked[:].rearrange("p i (c e) -> p c i e", e=4),
+            )
+            nc.vector.quantize_mx(
+                out=codes[:].bitcast(E5M2X4), scales=scales[:], in_=woven[:].rearrange("p j i -> p (j i)")
+            )
+            return codes, scales
+
+        def multiply(a, t, codes, scales):
+            nc.tensor.matmul_mx(
+                out=gq_ps[t][:],
+                lhsT=codes.bitcast(E5M2X4),
+                lhsT_scale=scales,
+                rhs=w_sb[:, a, :].bitcast(E2M1X4),
+                rhs_scale=w_sc[:, a, :],
+                start=(a == 0),
+                stop=(a == PASSES - 1),
+            )
+
+        picked = stage.tile([P, PACK, J], F32, name="picked_first", offset=4096, align_bytes=64)
+        woven = stage.tile([P, J, PACK], BF16, name="woven_first", offset=0, align_bytes=64)
+        for i in range(PACK):
+            gather(i % 2 == 1, picked[:, i, :], g_first[:, i, :].indirect(offsets[:]))
+        codes, scales = quantise(picked, woven, "first")
+        for t in range(TILES):
+            multiply(0, t, codes[:, t * P:(t + 1) * P], scales[:, t * P:(t + 1) * P])
+
+        planes = [g_pair[:, 0, :], g_pair[:, 1, :], g_lone[0][:], g_lone[1][:]]
+        picks = [stage.tile([P, PACK, P], F32, name=f"picked_{t}", offset=4096 + t * 2048, align_bytes=64) for t in range(TILES)]
+        for i in range(PACK):
             for t in range(TILES):
-                nc.vector.tensor_copy(
-                    out=woven[t][:].rearrange("p (c e) i -> p c i e", e=4),
-                    in_=picked[t][:].rearrange("p i (c e) -> p c i e", e=4),
-                )
-                nc.vector.quantize_mx(
-                    out=codes[t][:].bitcast(E5M2X4),
-                    scales=scales[t][:],
-                    in_=woven[t][:].rearrange("p j i -> p (j i)"),
-                )
-                nc.tensor.matmul_mx(
-                    out=gq_ps[t][:],
-                    lhsT=codes[t][:].bitcast(E5M2X4),
-                    lhsT_scale=scales[t][:],
-                    rhs=w_sb[:, a, :].bitcast(E2M1X4),
-                    rhs_scale=w_sc[:, a, :],
-                    start=(a == 0),
-                    stop=(a == PASSES - 1),
-                )
+                window = planes[i].indirect(offsets[:, t * tile_cols:(t + 1) * tile_cols])
+                gather(i == 2 or (i == 3 and t == 0), picks[t][:, i, :], window)
+        for t in range(TILES):
+            woven_t = stage.tile([P, P, PACK], BF16, name=f"woven_{t}", offset=(TILES - 1 - t) * 1024, align_bytes=64)
+            codes_t, scales_t = quantise(picks[t], woven_t, f"last{t}")
+            multiply(1, t, codes_t[:], scales_t[:])
         for t in range(TILES):
             nc.scalar.activation(out=gqi[t][:], in_=gq_ps[t][:], func=COPY, scale=inv_cols[:, t:t + 1])
 
@@ -115,10 +135,7 @@ def tile_list_unit_size_back_kernel(tc, g, w_words, w_scales, xh, inv, offs, out
             xj_t = [stage.tile([P, P], F32, name=f"xj_t{c}_{t}", offset=t * 512, align_bytes=64) for t in range(TILES)]
             for t in range(TILES):
                 window = xh_sb[c][:].indirect(offsets[:, t * tile_cols:(t + 1) * tile_cols])
-                if t < vector_tiles:
-                    nc.vector.tensor_copy(out=xj_t[t][:], in_=window)
-                else:
-                    nc.scalar.activation(out=xj_t[t][:], in_=window, func=COPY)
+                gather(t < vector_tiles, xj_t[t][:], window)
             for t in range(TILES):
                 nc.tensor.transpose(xj_ps[t][:, c * P:(c + 1) * P], xj_t[t][:], ident[:])
 
@@ -129,13 +146,13 @@ def tile_list_unit_size_back_kernel(tc, g, w_words, w_scales, xh, inv, offs, out
             )
 
         def total(t):
-            nc.vector.tensor_tensor(out=coef[:, t:t + 1], in0=early[:, t:t + 1], in1=parts[2][:, t:t + 1], op=ADD)
+            nc.scalar.activation(out=coef[:, t:t + 1], in_=parts[2][:, t:t + 1], func=IDENTITY, bias=early[:, t:t + 1])
 
-        def finish(t):
+        def finish(t, ks):
             nc.vector.scalar_tensor_tensor(
-                out=out_sb[t][:], in0=xj_ps[t][:], scalar=coef[:, t:t + 1], in1=gqi[t][:], op0=MULT, op1=ADD
+                out=out_sb[t][:, ks], in0=xj_ps[t][:, ks], scalar=coef[:, t:t + 1], in1=gqi[t][:, ks], op0=MULT, op1=ADD
             )
-            nc.sync.dma_start(out=out[t * P:(t + 1) * P, :], in_=out_sb[t][:])
+            nc.sync.dma_start(out=out[t * P:(t + 1) * P, ks], in_=out_sb[t][:, ks])
 
         bring(0, 4)
         bring(1, 2)
@@ -149,4 +166,8 @@ def tile_list_unit_size_back_kernel(tc, g, w_words, w_scales, xh, inv, offs, out
         for t in range(TILES):
             dot(t, slice(3 * P, 4 * P), parts[2])
             total(t)
-            finish(t)
+            if t < TILES - 1:
+                finish(t, slice(0, K))
+            else:
+                finish(t, slice(0, K // 2))
+                finish(t, slice(K // 2, K))

from contextlib import ExitStack

import concourse.mybir as mybir
from concourse.masks import make_identity

K, N, T, J = 512, 1024, 2048, 512
FLOPS = 2 * J * N * K

F32 = mybir.dt.float32
BF16 = mybir.dt.bfloat16
I32 = mybir.dt.int32
U32 = mybir.dt.uint32
U16 = mybir.dt.uint16
U8 = mybir.dt.uint8
E5M2X4 = mybir.dt.float8_e5m2_x4
E2M1X4 = mybir.dt.float4_e2m1fn_x4
MULT = mybir.AluOpType.mult
ADD = mybir.AluOpType.add
COPY = mybir.ActivationFunctionType.Copy
IDENTITY = mybir.ActivationFunctionType.Identity

P = 128
PACK = 4
PASSES = N // (P * PACK)
TILES = J // P
CHUNKS = K // P
HALF = J // 2
LIST_COLS = J // 16


def tile_list_unit_size_back_kernel(tc, g, w_words, w_scales, xh, inv, offs, out):
    nc = tc.nc
    with ExitStack() as ctx:
        keep = ctx.enter_context(tc.tile_pool(name="keep", bufs=1))
        stage = ctx.enter_context(tc.tile_pool(name="stage", bufs=1))
        psum = ctx.enter_context(tc.psum_pool(name="psum", bufs=1))

        offsets = keep.tile([P, LIST_COLS], U16, name="offsets")
        g_rows = g.rearrange("(a p i) t -> a p i t", a=PASSES, i=PACK)
        g_first = keep.tile([P, PACK, T], F32, name="g_first")
        g_pair = keep.tile([P, 2, T], F32, name="g_pair")
        g_lone = [keep.tile([P, T], F32, name=f"g_lone{u}") for u in range(2)]
        xh_sb = [keep.tile([P, T], F32, name=f"xh_{c}") for c in range(CHUNKS)]
        w_sb = keep.tile([P, PASSES, 2 * K], U8, name="w_sb", align_bytes=64)
        w_sc = keep.tile([P, PASSES, K], U8, name="w_sc", align_bytes=64)
        ident = keep.tile([P, P], F32, name="ident")
        inv_rows = keep.tile([P, P], F32, name="inv_rows")
        inv_cols = keep.tile([P, TILES], F32, name="inv_cols")

        nc.vector.memset(w_sc[:].bitcast(I32), 0)
        nc.vector.memset(inv_rows[:], 0.0)
        make_identity(nc, ident[:])

        nc.sync.dma_start(out=g_first[:], in_=g_rows[0])
        nc.sync.dma_start(offsets[:], offs)
        nc.sync.dma_start(out=g_pair[:], in_=g_rows[1, :, 0:2, :])
        nc.sync.dma_start(out=inv_rows[0:TILES, :], in_=inv.rearrange("(t p) o -> t (p o)", p=P))
        for q in range(4):
            nc.sync.dma_start(
                out=w_sc[32 * q:32 * q + 4, :, :].bitcast(I32),
                in_=w_scales[:, 4 * q:4 * q + 4, :].rearrange("z r c -> r z c").bitcast(I32),
            )
        nc.sync.dma_start(out=w_sb[:].bitcast(I32), in_=w_words.rearrange("z p b -> p z b").bitcast(I32))
        for u in range(2):
            nc.sync.dma_start(out=g_lone[u][:], in_=g_rows[1, :, 2 + u, :])
        for c in range(CHUNKS):
            nc.sync.dma_start(out=xh_sb[c][:], in_=xh[c * P:(c + 1) * P, :])

        gq_ps = [psum.tile([P, K], F32, name=f"gq_ps{t}") for t in range(TILES)]
        xj_ps = [psum.tile([P, K], F32, name=f"xj_ps{t}") for t in range(TILES)]

        nc.tensor.transpose(xj_ps[0][:, 0:P], inv_rows[:], ident[:])
        nc.vector.tensor_copy(out=inv_cols[:], in_=xj_ps[0][:, 0:TILES])

        gqi = [keep.tile([P, K], F32, name=f"gqi{t}") for t in range(TILES)]
        tile_cols = LIST_COLS // TILES

        def gather(on_vector, dst, window):
            if on_vector:
                nc.vector.tensor_copy(out=dst, in_=window)
            else:
                nc.scalar.activation(out=dst, in_=window, func=COPY)

        def quantise(picked, woven, name):
            width = woven.shape[1]
            codes = keep.tile([P, width], U32, name=f"codes_{name}", align_bytes=64)
            scales = keep.tile([P, width], U8, name=f"scales_{name}", align_bytes=64)
            nc.vector.tensor_copy(
                out=woven[:].rearrange("p (c e) i -> p c i e", e=4),
                in_=picked[:].rearrange("p i (c e) -> p c i e", e=4),
            )
            nc.vector.quantize_mx(
                out=codes[:].bitcast(E5M2X4), scales=scales[:], in_=woven[:].rearrange("p j i -> p (j i)")
            )
            return codes, scales

        def multiply(a, t, codes, scales):
            nc.tensor.matmul_mx(
                out=gq_ps[t][:],
                lhsT=codes.bitcast(E5M2X4),
                lhsT_scale=scales,
                rhs=w_sb[:, a, :].bitcast(E2M1X4),
                rhs_scale=w_sc[:, a, :],
                start=(a == 0),
                stop=(a == PASSES - 1),
            )

        picked = stage.tile([P, PACK, J], F32, name="picked_first", offset=4096, align_bytes=64)
        woven = stage.tile([P, J, PACK], BF16, name="woven_first", offset=0, align_bytes=64)
        for i in range(PACK):
            gather(i % 2 == 1, picked[:, i, :], g_first[:, i, :].indirect(offsets[:]))
        codes, scales = quantise(picked, woven, "first")
        for t in range(TILES):
            multiply(0, t, codes[:, t * P:(t + 1) * P], scales[:, t * P:(t + 1) * P])

        planes = [g_pair[:, 0, :], g_pair[:, 1, :], g_lone[0][:], g_lone[1][:]]
        picks = [stage.tile([P, PACK, P], F32, name=f"picked_{t}", offset=4096 + t * 2048, align_bytes=64) for t in range(TILES)]
        for i in range(PACK):
            for t in range(TILES):
                window = planes[i].indirect(offsets[:, t * tile_cols:(t + 1) * tile_cols])
                gather(i == 2 or (i == 3 and t == 0), picks[t][:, i, :], window)
        for t in range(TILES):
            woven_t = stage.tile([P, P, PACK], BF16, name=f"woven_{t}", offset=(TILES - 1 - t) * 1024, align_bytes=64)
            codes_t, scales_t = quantise(picks[t], woven_t, f"last{t}")
            multiply(1, t, codes_t[:], scales_t[:])
        for t in range(TILES):
            nc.scalar.activation(out=gqi[t][:], in_=gq_ps[t][:], func=COPY, scale=inv_cols[:, t:t + 1])

        out_sb = [keep.tile([P, K], F32, name=f"out_sb{t}") for t in range(TILES)]
        parts = [keep.tile([P, TILES], F32, name=f"parts{n}") for n in range(3)]
        early = keep.tile([P, TILES], F32, name="early")
        coef = keep.tile([P, TILES], F32, name="coef")

        def bring(c, vector_tiles):
            xj_t = [stage.tile([P, P], F32, name=f"xj_t{c}_{t}", offset=t * 512, align_bytes=64) for t in range(TILES)]
            for t in range(TILES):
                window = xh_sb[c][:].indirect(offsets[:, t * tile_cols:(t + 1) * tile_cols])
                gather(t < vector_tiles, xj_t[t][:], window)
            for t in range(TILES):
                nc.tensor.transpose(xj_ps[t][:, c * P:(c + 1) * P], xj_t[t][:], ident[:])

        def dot(t, ks, part):
            nc.vector.scalar_tensor_tensor(
                out=out_sb[t][:, ks], in0=xj_ps[t][:, ks], scalar=-1.0 / K, in1=gqi[t][:, ks],
                op0=MULT, op1=MULT, accum_out=part[:, t:t + 1],
            )

        def total(t):
            nc.scalar.activation(out=coef[:, t:t + 1], in_=parts[2][:, t:t + 1], func=IDENTITY, bias=early[:, t:t + 1])

        def finish(t, ks):
            nc.vector.scalar_tensor_tensor(
                out=out_sb[t][:, ks], in0=xj_ps[t][:, ks], scalar=coef[:, t:t + 1], in1=gqi[t][:, ks], op0=MULT, op1=ADD
            )
            nc.sync.dma_start(out=out[t * P:(t + 1) * P, ks], in_=out_sb[t][:, ks])

        bring(0, 4)
        bring(1, 2)
        for t in range(TILES):
            dot(t, slice(0, 2 * P), parts[0])
        bring(2, 0)
        for t in range(TILES):
            dot(t, slice(2 * P, 3 * P), parts[1])
        nc.vector.tensor_tensor(out=early[:], in0=parts[0][:], in1=parts[1][:], op=ADD)
        bring(3, 0)
        for t in range(TILES):
            dot(t, slice(3 * P, 4 * P), parts[2])
            total(t)
            if t < TILES - 1:
                finish(t, slice(0, K))
            else:
                finish(t, slice(0, K // 2))
                finish(t, slice(K // 2, K))
